import numpy as np
import ml_dtypes


def mxq(x, axis, fmt="e4m3"):
    dtype, down = {"e4m3": (ml_dtypes.float8_e4m3fn, 7), "e5m2": (ml_dtypes.float8_e5m2, 14)}[fmt]
    v = np.moveaxis(np.asarray(x, np.float32).astype(ml_dtypes.bfloat16).astype(np.float64), axis, -1)
    blocks = v.reshape(v.shape[:-1] + (-1, 32))
    amax = np.abs(blocks).max(-1, keepdims=True)
    byte = np.maximum(np.where(amax > 0, np.frexp(amax)[1] - 1 + 127, 0) - down, 1)
    scale = np.exp2(byte - 127.0)
    codes = (blocks / scale).astype(np.float32).astype(dtype).astype(np.float64)
    return np.moveaxis((codes * scale).reshape(v.shape), -1, axis)


WIDE = False


def mx_kscale(k):
    if not WIDE:
        return np.ones(k)
    levels = np.array([10, -10, 5, -5, 0])
    if k % 512:
        return np.exp2(np.random.permutation(np.resize(levels, k // 32))).repeat(32)
    a = np.empty((k // 512, 16))
    for p in range(k // 512):
        a[p, :8] = np.random.permutation(np.resize(levels, 8))
        for g in range(8):
            far = levels[np.abs(levels - a[p, g]) >= 10]
            a[p, g + 8] = far[np.random.randint(len(far))]
    return np.exp2(a.ravel()).repeat(32)


def f64(x):
    return np.asarray(x).astype(np.float64)


def striped(idx):
    return np.tile(np.asarray(idx).reshape(-1, 16).T, (8, 1)).astype(np.uint16)


def unstriped(offs):
    return offs[:16].T.reshape(-1).astype(np.int64)


E2M1 = np.array([0.0, 0.5, 1.0, 1.5, 2.0, 3.0, 4.0, 6.0, -0.0, -0.5, -1.0, -1.5, -2.0, -3.0, -4.0, -6.0])


def pack_weight(w, fmt):
    k, n = w.shape
    w = f64(np.asarray(w, np.float32).astype(ml_dtypes.bfloat16)).reshape(k // 32, 32, n)
    amax = np.abs(w).max(1)
    if fmt == "e4m3":
        byte = np.frexp(amax)[1] - 1 + 127 - 7
    else:
        mant, ex = np.frexp(amax / 6.0)
        byte = np.where(mant > 0.5, ex, ex - 1) + 127
    byte = np.clip(np.where(amax > 0, byte, 1), 1, 254)
    scaled = (w * np.exp2(127.0 - byte)[:, None, :]).reshape(k, n).astype(np.float32)
    by_word = np.ascontiguousarray(scaled.reshape(k // 512, 128, 4, n).transpose(0, 1, 3, 2))
    if fmt == "e4m3":
        words = by_word.astype(ml_dtypes.float8_e4m3fn).view(np.uint8)
    else:
        c = by_word.astype(ml_dtypes.float4_e2m1fn).view(np.uint8) & 0xF
        words = (c[..., 0::2] | (c[..., 1::2] << 4)).reshape(k // 512, 128, 2 * n)
    return np.ascontiguousarray(words), np.ascontiguousarray(byte.astype(np.uint8).reshape(k // 512, 16, n))


def unpack_weight(words, scales, fmt):
    g, _, n = scales.shape
    words = np.ascontiguousarray(words).reshape(g, 128, n, -1)
    if fmt == "e4m3":
        vals = words.view(ml_dtypes.float8_e4m3fn).astype(np.float64)
    else:
        nib = np.empty((g, 128, n, 4), np.uint8)
        nib[..., 0::2] = words & 0xF
        nib[..., 1::2] = words >> 4
        vals = E2M1[nib]
    vals = vals * np.repeat(np.exp2(scales.astype(np.float64) - 127.0), 8, axis=1)[..., None]
    return vals.transpose(0, 1, 3, 2).reshape(g * 512, n)


D, E, T, I, G, U, Q = 512, 512, 4096, 1024, 64, 512, 128


def setup_inputs():
    n = np.random.standard_normal
    idx = np.random.permutation(T)[:I]
    idx2 = np.repeat(np.random.permutation(U)[:G], I // G)
    idx3 = idx2[:: I // G]
    fd = mx_kscale(D)
    fe = mx_kscale(E)
    keysp = pack_weight(n((D, T)) / fd[:, None], "e2m1")
    valsp = pack_weight(n((E, T)) / fe[:, None], "e2m1")
    return {
        "query": (n((D, Q)) * 0.5 / np.sqrt(D) * fd[:, None]).astype(np.float32),
        "keys_words": keysp[0],
        "keys_scales": keysp[1],
        "kscale": np.tile(np.random.uniform(0.5, 2.0, U), (128, 1)).astype(np.float32),
        "gout": (n((E, Q)) * 1 / np.sqrt(E) * fe[:, None]).astype(np.float32),
        "vals_words": valsp[0],
        "vals_scales": valsp[1],
        "lse": (np.random.uniform(6.8, 7.2, (Q, 1))).astype(np.float32),
        "delta": (np.random.uniform(-0.3, 0.3, (Q, 1))).astype(np.float32),
        "old": (2.0 * n((Q, U))).astype(np.float32),
        "offs": striped(idx),
        "offs2": striped(idx2),
        "offs3": striped(idx3),
    }


def reference(query, keys_words, keys_scales, kscale, gout, vals_words, vals_scales, lse, delta, old, offs, offs2, offs3):
    idx = unstriped(offs)
    idx2 = unstriped(offs2)
    idx3 = unstriped(offs3)
    keysu = unpack_weight(keys_words, keys_scales, "e2m1")
    valsu = unpack_weight(vals_words, vals_scales, "e2m1")
    queryq = mxq(f64(query), 0, "e4m3")
    keysidxg = keysu[:, idx]
    a = queryq.T @ keysidxg
    goutq = mxq(f64(gout), 0, "e4m3")
    valsidxg = valsu[:, idx]
    dp = goutq.T @ valsidxg
    ds = np.exp(a * f64(kscale)[:1][:, idx2] - f64(lse)) * (dp - f64(delta)) * a * 512.0
    gk = ds.reshape(Q, G, I // G).sum(axis=2)
    gf = np.zeros((Q, U))
    gf[:, idx3] = gk
    y = f64(old) + gf
    return y

@@ -1,0 +1,134 @@
+from contextlib import ExitStack
+
+import concourse.mybir as mybir
+
+F32 = mybir.dt.float32
+BF16 = mybir.dt.bfloat16
+I32 = mybir.dt.int32
+U32 = mybir.dt.uint32
+U16 = mybir.dt.uint16
+U8 = mybir.dt.uint8
+FP8X4 = mybir.dt.float8_e4m3fn_x4
+FP4X4 = mybir.dt.float4_e2m1fn_x4
+ACT = mybir.ActivationFunctionType
+ALU = mybir.AluOpType
+AX = mybir.AxisListType
+
+P = 128
+T = 4096
+SLOTS = 1024
+HALF = 512
+PAGE = 16
+PAGES = 64
+U = 512
+Q = 128
+FLOPS = 2 * 2 * 512 * Q * SLOTS
+
+
+def tile_attend_gpagescale_kernel(tc, query, keys_words, keys_scales, kscale, gout, vals_words, vals_scales, lse, delta, old, offs, offs2, offs3, out):
+    nc = tc.nc
+    with ExitStack() as ctx:
+        sb = ctx.enter_context(tc.tile_pool(name="sb", bufs=1))
+        ps = ctx.enter_context(tc.psum_pool(name="ps", bufs=1))
+
+        def tile(name, shape, dtype):
+            return sb.tile(shape, dtype, name=name, align_bytes=64)
+
+        l1 = tile("l1", [P, SLOTS // 16], U16)
+        l2 = tile("l2", [P, SLOTS // 16], U16)
+        l3 = tile("l3", [P, PAGES // 16], U16)
+        ksc = tile("ksc", [P, U], F32)
+        kw = tile("kw", [P, T], U16)
+        vw = tile("vw", [P, T], U16)
+        kb = tile("kb", [P, T], U8)
+        vb = tile("vb", [P, T], U8)
+        qraw = tile("qraw", [P, 4, Q], F32)
+        graw = tile("graw", [P, 4, Q], F32)
+        lse_t = tile("lse_t", [P, 1], F32)
+        del_t = tile("del_t", [P, 1], F32)
+        nlse = tile("nlse", [P, 1], F32)
+        old_t = tile("old_t", [P, U], F32)
+        gf = tile("gf", [P, U], F32)
+        warm = tile("warm", [P, 1], F32)
+        warm2 = tile("warm2", [P, 1], F32)
+
+        nc.vector.memset(kb[:].bitcast(I32), 0)
+        nc.gpsimd.memset(warm[:], 0.0)
+        nc.scalar.activation(warm2[:], warm[:], ACT.Exp)
+        nc.vector.memset(vb[:].bitcast(I32), 0)
+        nc.gpsimd.memset(gf[:], 0.0)
+
+        def load_bytes(dst, src, eng):
+            for r in range(4):
+                eng.dma_start(dst[r:P:32, :].bitcast(I32), src[0, r:16:4, :].bitcast(I32))
+
+        nc.sync.dma_start(l2[:], offs2)
+        nc.sync.dma_start(ksc[:], kscale)
+        nc.sync.dma_start(l1[:], offs)
+        nc.sync.dma_start(l3[:], offs3)
+        load_bytes(kb, keys_scales, nc.sync)
+        nc.sync.dma_start(kw[:].bitcast(I32), keys_words[0].bitcast(I32))
+        nc.sync.dma_start(qraw[:], query.rearrange("(p j) w -> p j w", j=4))
+        nc.sync.dma_start(lse_t[:], lse)
+        load_bytes(vb, vals_scales, nc.sync)
+        nc.sync.dma_start(graw[:], gout.rearrange("(p j) w -> p j w", j=4))
+        nc.sync.dma_start(vw[:].bitcast(I32), vals_words[0].bitcast(I32))
+        nc.sync.dma_start(del_t[:], delta)
+        nc.sync.dma_start(old_t[:], old)
+
+        nc.scalar.mul(nlse[:], lse_t[:], -1.0)
+
+        kg = tile("kg", [P, SLOTS], F32)
+        for c in range(4):
+            nc.vector.tensor_copy(kg[:, 256 * c : 256 * (c + 1)], ksc[:].indirect(l2[:, 16 * c : 16 * (c + 1)]))
+
+        def quantise(name, raw):
+            bf = tile(name + "_bf", [P, Q, 4], BF16)
+            nc.scalar.copy(bf[:], raw[:].rearrange("p j w -> p w j"))
+            codes = tile(name + "_codes", [P, Q], U32)
+            scales = tile(name + "_scales", [P, Q], U8)
+            nc.vector.quantize_mx(out=codes[:].bitcast(FP8X4), scales=scales[:], in_=bf[:].rearrange("p w j -> p (w j)"))
+            return codes, scales
+
+        def gather(name, window, dtype, h, n):
+            g = tile(name, [P, n], dtype)
+            nc.vector.tensor_copy(g[:], window[:].indirect(l1[:, h * HALF // 16 : (h * HALF + n) // 16]))
+            return g
+
+        def product(name, codes, scales, words, plane):
+            acc = ps.tile([P, HALF], F32, name=name)
+            nc.tensor.matmul_mx(out=acc[:], lhsT=codes[:].bitcast(FP8X4), lhsT_scale=scales[:], rhs=words.bitcast(FP4X4), rhs_scale=plane, start=True, stop=True)
+            return acc
+
+        kbg = gather("kbg", kb, U8, 0, SLOTS)
+        qc, qs = quantise("q", qraw)
+        a, e, w = [], [], []
+        for h in range(2):
+            kwg = gather("kwg%d" % h, kw, U16, h, HALF)
+            acc = product("a%d" % h, qc, qs, kwg[:], kbg[:, h * HALF : (h + 1) * HALF])
+            a.append(tile("asb%d" % h, [P, HALF], F32))
+            nc.scalar.copy(a[h][:], acc[:])
+            e.append(tile("e%d" % h, [P, HALF], F32))
+            for g in range(HALF // PAGE):
+                col = h * HALF + g * PAGE
+                nc.scalar.activation(e[h][:, g * PAGE : (g + 1) * PAGE], a[h][:, g * PAGE : (g + 1) * PAGE], ACT.Exp, bias=nlse[:], scale=kg[:, col : col + 1])
+        gc, gs = quantise("g", graw)
+        vbg = gather("vbg", vb, U8, 0, SLOTS)
+        dp = []
+        for h in range(2):
+            vwg = gather("vwg%d" % h, vw, U16, h, HALF)
+            dp.append(product("dp%d" % h, gc, gs, vwg[:], vbg[:, h * HALF : (h + 1) * HALF]))
+        gk = tile("gk", [P, PAGES], F32)
+        for h in range(2):
+            ds = tile("ds%d" % h, [P, HALF], F32)
+            v = tile("v%d" % h, [P, HALF], F32)
+            nc.vector.scalar_tensor_tensor(v[:], dp[h][:], del_t[:], a[h][:], ALU.subtract, ALU.mult)
+            nc.vector.tensor_tensor(ds[:], v[:], e[h][:], ALU.mult)
+            nc.vector.tensor_reduce(gk[:, h * 32 : (h + 1) * 32], ds[:].rearrange("p (g j) -> p g j", j=PAGE), AX.X, ALU.add)
+
+        nc.vector.tensor_copy(gf[:].indirect(l3[:]), gk[:])
+        for h, eng in enumerate((nc.sync, nc.scalar)):
+            cols = slice(h * U // 2, (h + 1) * U // 2)
+            res = tile("res%d" % h, [P, U // 2], F32)
+            nc.vector.scalar_tensor_tensor(res[:], gf[:, cols], 512.0, old_t[:, cols], ALU.mult, ALU.add)
+            eng.dma_start(out[:, cols], res[:])

@@ -62,18 +62,18 @@ def tile_attend_gpagescale_kernel(tc, query, keys_words, keys_scales, kscale, go
             for r in range(4):
                 eng.dma_start(dst[r:P:32, :].bitcast(I32), src[0, r:16:4, :].bitcast(I32))
 
+        nc.scalar.dma_start(ksc[:], kscale)
         nc.sync.dma_start(l2[:], offs2)
-        nc.sync.dma_start(ksc[:], kscale)
         nc.sync.dma_start(l1[:], offs)
-        nc.sync.dma_start(l3[:], offs3)
         load_bytes(kb, keys_scales, nc.sync)
-        nc.sync.dma_start(kw[:].bitcast(I32), keys_words[0].bitcast(I32))
         nc.sync.dma_start(qraw[:], query.rearrange("(p j) w -> p j w", j=4))
+        nc.sync.dma_start(kw[:].bitcast(I32), keys_words[0].bitcast(I32))
+        nc.sync.dma_start(graw[:], gout.rearrange("(p j) w -> p j w", j=4))
         nc.sync.dma_start(lse_t[:], lse)
         load_bytes(vb, vals_scales, nc.sync)
-        nc.sync.dma_start(graw[:], gout.rearrange("(p j) w -> p j w", j=4))
         nc.sync.dma_start(vw[:].bitcast(I32), vals_words[0].bitcast(I32))
         nc.sync.dma_start(del_t[:], delta)
+        nc.sync.dma_start(l3[:], offs3)
         nc.sync.dma_start(old_t[:], old)
 
         nc.scalar.mul(nlse[:], lse_t[:], -1.0)
@@ -102,29 +102,32 @@ def tile_attend_gpagescale_kernel(tc, query, keys_words, keys_scales, kscale, go
 
         kbg = gather("kbg", kb, U8, 0, SLOTS)
         qc, qs = quantise("q", qraw)
-        a, e, w = [], [], []
+        gc, gs = quantise("g", graw)
+        w = []
         for h in range(2):
             kwg = gather("kwg%d" % h, kw, U16, h, HALF)
             acc = product("a%d" % h, qc, qs, kwg[:], kbg[:, h * HALF : (h + 1) * HALF])
-            a.append(tile("asb%d" % h, [P, HALF], F32))
-            nc.scalar.copy(a[h][:], acc[:])
-            e.append(tile("e%d" % h, [P, HALF], F32))
-            for g in range(HALF // PAGE):
-                col = h * HALF + g * PAGE
-                nc.scalar.activation(e[h][:, g * PAGE : (g + 1) * PAGE], a[h][:, g * PAGE : (g + 1) * PAGE], ACT.Exp, bias=nlse[:], scale=kg[:, col : col + 1])
-        gc, gs = quantise("g", graw)
+            a = tile("asb%d" % h, [P, HALF], F32)
+            nc.scalar.copy(a[:], acc[:])
+            t = tile("t%d" % h, [P, HALF], F32)
+            nc.gpsimd.tensor_tensor(t[:], a[:], kg[:, h * HALF : (h + 1) * HALF], ALU.mult)
+            e = tile("e%d" % h, [P, HALF], F32)
+            nc.scalar.activation(e[:], t[:], ACT.Exp, bias=nlse[:])
+            w.append(tile("w%d" % h, [P, HALF], F32))
+            nc.gpsimd.tensor_tensor(w[h][:], a[:], e[:], ALU.mult)
         vbg = gather("vbg", vb, U8, 0, SLOTS)
-        dp = []
-        for h in range(2):
-            vwg = gather("vwg%d" % h, vw, U16, h, HALF)
-            dp.append(product("dp%d" % h, gc, gs, vwg[:], vbg[:, h * HALF : (h + 1) * HALF]))
         gk = tile("gk", [P, PAGES], F32)
+        vwg = [gather("vwg%d" % h, vw, U16, h, HALF) for h in range(2)]
+        ds = []
         for h in range(2):
-            ds = tile("ds%d" % h, [P, HALF], F32)
-            v = tile("v%d" % h, [P, HALF], F32)
-            nc.vector.scalar_tensor_tensor(v[:], dp[h][:], del_t[:], a[h][:], ALU.subtract, ALU.mult)
-            nc.vector.tensor_tensor(ds[:], v[:], e[h][:], ALU.mult)
-            nc.vector.tensor_reduce(gk[:, h * 32 : (h + 1) * 32], ds[:].rearrange("p (g j) -> p g j", j=PAGE), AX.X, ALU.add)
+            ds.append(tile("ds%d" % h, [P, HALF], F32))
+            n = HALF // (h + 1)
+            for c in range(0, HALF, n):
+                dp = ps.tile([P, n], F32, name="dp%d_%d" % (h, c))
+                nc.tensor.matmul_mx(out=dp[:], lhsT=gc[:].bitcast(FP8X4), lhsT_scale=gs[:], rhs=vwg[h][:, c : c + n].bitcast(FP4X4), rhs_scale=vbg[:, h * HALF + c : h * HALF + c + n], start=True, stop=True)
+                nc.vector.scalar_tensor_tensor(ds[h][:, c : c + n], dp[:], del_t[:], w[h][:, c : c + n], ALU.subtract, ALU.mult)
+        for h in range(2):
+            nc.vector.tensor_reduce(gk[:, h * 32 : (h + 1) * 32], ds[h][:].rearrange("p (g j) -> p g j", j=PAGE), AX.X, ALU.add)
 
         nc.vector.tensor_copy(gf[:].indirect(l3[:]), gk[:])
         for h, eng in enumerate((nc.sync, nc.scalar)):

from contextlib import ExitStack

import concourse.mybir as mybir

F32 = mybir.dt.float32
BF16 = mybir.dt.bfloat16
I32 = mybir.dt.int32
U32 = mybir.dt.uint32
U16 = mybir.dt.uint16
U8 = mybir.dt.uint8
FP8X4 = mybir.dt.float8_e4m3fn_x4
FP4X4 = mybir.dt.float4_e2m1fn_x4
ACT = mybir.ActivationFunctionType
ALU = mybir.AluOpType
AX = mybir.AxisListType

P = 128
T = 4096
SLOTS = 1024
HALF = 512
PAGE = 16
PAGES = 64
U = 512
Q = 128
FLOPS = 2 * 2 * 512 * Q * SLOTS


def tile_attend_gpagescale_kernel(tc, query, keys_words, keys_scales, kscale, gout, vals_words, vals_scales, lse, delta, old, offs, offs2, offs3, out):
    nc = tc.nc
    with ExitStack() as ctx:
        sb = ctx.enter_context(tc.tile_pool(name="sb", bufs=1))
        ps = ctx.enter_context(tc.psum_pool(name="ps", bufs=1))

        def tile(name, shape, dtype):
            return sb.tile(shape, dtype, name=name, align_bytes=64)

        l1 = tile("l1", [P, SLOTS // 16], U16)
        l2 = tile("l2", [P, SLOTS // 16], U16)
        l3 = tile("l3", [P, PAGES // 16], U16)
        ksc = tile("ksc", [P, U], F32)
        kw = tile("kw", [P, T], U16)
        vw = tile("vw", [P, T], U16)
        kb = tile("kb", [P, T], U8)
        vb = tile("vb", [P, T], U8)
        qraw = tile("qraw", [P, 4, Q], F32)
        graw = tile("graw", [P, 4, Q], F32)
        lse_t = tile("lse_t", [P, 1], F32)
        del_t = tile("del_t", [P, 1], F32)
        nlse = tile("nlse", [P, 1], F32)
        old_t = tile("old_t", [P, U], F32)
        gf = tile("gf", [P, U], F32)
        warm = tile("warm", [P, 1], F32)
        warm2 = tile("warm2", [P, 1], F32)

        nc.vector.memset(kb[:].bitcast(I32), 0)
        nc.gpsimd.memset(warm[:], 0.0)
        nc.scalar.activation(warm2[:], warm[:], ACT.Exp)
        nc.vector.memset(vb[:].bitcast(I32), 0)
        nc.gpsimd.memset(gf[:], 0.0)

        def load_bytes(dst, src, eng):
            for r in range(4):
                eng.dma_start(dst[r:P:32, :].bitcast(I32), src[0, r:16:4, :].bitcast(I32))

        nc.scalar.dma_start(ksc[:], kscale)
        nc.sync.dma_start(l2[:], offs2)
        nc.sync.dma_start(l1[:], offs)
        load_bytes(kb, keys_scales, nc.sync)
        nc.sync.dma_start(qraw[:], query.rearrange("(p j) w -> p j w", j=4))
        nc.sync.dma_start(kw[:].bitcast(I32), keys_words[0].bitcast(I32))
        nc.sync.dma_start(graw[:], gout.rearrange("(p j) w -> p j w", j=4))
        nc.sync.dma_start(lse_t[:], lse)
        load_bytes(vb, vals_scales, nc.sync)
        nc.sync.dma_start(vw[:].bitcast(I32), vals_words[0].bitcast(I32))
        nc.sync.dma_start(del_t[:], delta)
        nc.sync.dma_start(l3[:], offs3)
        nc.sync.dma_start(old_t[:], old)

        nc.scalar.mul(nlse[:], lse_t[:], -1.0)

        kg = tile("kg", [P, SLOTS], F32)
        for c in range(4):
            nc.vector.tensor_copy(kg[:, 256 * c : 256 * (c + 1)], ksc[:].indirect(l2[:, 16 * c : 16 * (c + 1)]))

        def quantise(name, raw):
            bf = tile(name + "_bf", [P, Q, 4], BF16)
            nc.scalar.copy(bf[:], raw[:].rearrange("p j w -> p w j"))
            codes = tile(name + "_codes", [P, Q], U32)
            scales = tile(name + "_scales", [P, Q], U8)
            nc.vector.quantize_mx(out=codes[:].bitcast(FP8X4), scales=scales[:], in_=bf[:].rearrange("p w j -> p (w j)"))
            return codes, scales

        def gather(name, window, dtype, h, n):
            g = tile(name, [P, n], dtype)
            nc.vector.tensor_copy(g[:], window[:].indirect(l1[:, h * HALF // 16 : (h * HALF + n) // 16]))
            return g

        def product(name, codes, scales, words, plane):
            acc = ps.tile([P, HALF], F32, name=name)
            nc.tensor.matmul_mx(out=acc[:], lhsT=codes[:].bitcast(FP8X4), lhsT_scale=scales[:], rhs=words.bitcast(FP4X4), rhs_scale=plane, start=True, stop=True)
            return acc

        kbg = gather("kbg", kb, U8, 0, SLOTS)
        qc, qs = quantise("q", qraw)
        gc, gs = quantise("g", graw)
        w = []
        for h in range(2):
            kwg = gather("kwg%d" % h, kw, U16, h, HALF)
            acc = product("a%d" % h, qc, qs, kwg[:], kbg[:, h * HALF : (h + 1) * HALF])
            a = tile("asb%d" % h, [P, HALF], F32)
            nc.scalar.copy(a[:], acc[:])
            t = tile("t%d" % h, [P, HALF], F32)
            nc.gpsimd.tensor_tensor(t[:], a[:], kg[:, h * HALF : (h + 1) * HALF], ALU.mult)
            e = tile("e%d" % h, [P, HALF], F32)
            nc.scalar.activation(e[:], t[:], ACT.Exp, bias=nlse[:])
            w.append(tile("w%d" % h, [P, HALF], F32))
            nc.gpsimd.tensor_tensor(w[h][:], a[:], e[:], ALU.mult)
        vbg = gather("vbg", vb, U8, 0, SLOTS)
        gk = tile("gk", [P, PAGES], F32)
        vwg = [gather("vwg%d" % h, vw, U16, h, HALF) for h in range(2)]
        ds = []
        for h in range(2):
            ds.append(tile("ds%d" % h, [P, HALF], F32))
            n = HALF // (h + 1)
            for c in range(0, HALF, n):
                dp = ps.tile([P, n], F32, name="dp%d_%d" % (h, c))
                nc.tensor.matmul_mx(out=dp[:], lhsT=gc[:].bitcast(FP8X4), lhsT_scale=gs[:], rhs=vwg[h][:, c : c + n].bitcast(FP4X4), rhs_scale=vbg[:, h * HALF + c : h * HALF + c + n], start=True, stop=True)
                nc.vector.scalar_tensor_tensor(ds[h][:, c : c + n], dp[:], del_t[:], w[h][:, c : c + n], ALU.subtract, ALU.mult)
        for h in range(2):
            nc.vector.tensor_reduce(gk[:, h * 32 : (h + 1) * 32], ds[h][:].rearrange("p (g j) -> p g j", j=PAGE), AX.X, ALU.add)

        nc.vector.tensor_copy(gf[:].indirect(l3[:]), gk[:])
        for h, eng in enumerate((nc.sync, nc.scalar)):
            cols = slice(h * U // 2, (h + 1) * U // 2)
            res = tile("res%d" % h, [P, U // 2], F32)
            nc.vector.scalar_tensor_tensor(res[:], gf[:, cols], 512.0, old_t[:, cols], ALU.mult, ALU.add)
            eng.dma_start(out[:, cols], res[:])
